import numpy as np
import ml_dtypes


def mxq(x, axis, fmt="e4m3"):
    dtype, down = {"e4m3": (ml_dtypes.float8_e4m3fn, 7), "e5m2": (ml_dtypes.float8_e5m2, 14)}[fmt]
    v = np.moveaxis(np.asarray(x, np.float32).astype(ml_dtypes.bfloat16).astype(np.float64), axis, -1)
    blocks = v.reshape(v.shape[:-1] + (-1, 32))
    amax = np.abs(blocks).max(-1, keepdims=True)
    byte = np.maximum(np.where(amax > 0, np.frexp(amax)[1] - 1 + 127, 0) - down, 1)
    scale = np.exp2(byte - 127.0)
    codes = (blocks / scale).astype(np.float32).astype(dtype).astype(np.float64)
    return np.moveaxis((codes * scale).reshape(v.shape), -1, axis)


WIDE = False


def mx_kscale(k, group=512):
    if not WIDE:
        return np.ones(k)
    levels = np.array([10, -10, 5, -5, 0])
    if group != 512:
        return np.exp2(np.random.permutation(np.resize(levels, k // group))).repeat(group)
    if k % 512:
        return np.exp2(np.random.permutation(np.resize(levels, k // 32))).repeat(32)
    a = np.empty((k // 512, 16))
    for p in range(k // 512):
        a[p, :8] = np.random.permutation(np.resize(levels, 8))
        for g in range(8):
            far = levels[np.abs(levels - a[p, g]) >= 10]
            a[p, g + 8] = far[np.random.randint(len(far))]
    return np.exp2(a.ravel()).repeat(32)


def f64(x):
    return np.asarray(x).astype(np.float64)


G, D, M, O, N = 2, 256, 256, 256, 512


def sgn(shape):
    return np.random.uniform(0.5, 2.0, shape) * np.where(np.random.standard_normal(shape) < 0, -1.0, 1.0)


def setup_inputs():
    n = np.random.standard_normal
    s_d = mx_kscale(D, 0)
    s_m = mx_kscale(M, 0)
    return {
        "x": (n((G, D, N)) * s_d[:, None]).astype(np.float32),
        "w1": (n((G, D, M)) / np.sqrt(D) / s_d[:, None]).astype(np.float32),
        "w2": (n((G, D, M)) / np.sqrt(D) / s_d[:, None]).astype(np.float32),
        "tp": (np.random.uniform(0.5, 1.2, (G, M, 1))).astype(np.float32),
        "hs": (sgn((G, M, 1)) * s_m[:, None]).astype(np.float32),
        "wo2": (n((G, M, O)) / np.sqrt(M) / s_m[:, None]).astype(np.float32),
        "ob": (0.5 * n((G, O, 1))).astype(np.float32),
        "osc": (np.random.uniform(0.5, 2.0, (G, O, 1))).astype(np.float32),
    }


def reference(x, w1, w2, tp, hs, wo2, ob, osc):
    w1q = mxq(f64(w1), 1, "e4m3")
    xq = mxq(f64(x), 1, "e4m3")
    z1 = w1q.transpose(0, 2, 1) @ xq
    w2q = mxq(f64(w2), 1, "e4m3")
    z2 = w2q.transpose(0, 2, 1) @ xq
    p1 = np.exp(z1 * f64(tp) - np.max(z1 * f64(tp), axis=-1, keepdims=True))
    zs = np.sum(p1, axis=-1, keepdims=True)
    h = p1 / zs * z2 * 512.0
    hh = h * f64(hs)
    wo2q = mxq(f64(wo2), 1, "e4m3")
    hhq = mxq(hh, 1, "e4m3")
    y0 = wo2q.transpose(0, 2, 1) @ hhq
    y = np.tanh(y0 + f64(ob)) * f64(osc)
    return y

@@ -1,0 +1,214 @@
+from contextlib import ExitStack
+
+import concourse.mybir as mybir
+
+G, D, M, O, N = 2, 256, 256, 256, 512
+FLOPS = 2 * G * N * (2 * D * M + M * O)
+
+F32 = mybir.dt.float32
+BF16 = mybir.dt.bfloat16
+U32 = mybir.dt.uint32
+U8 = mybir.dt.uint8
+FP8X4 = mybir.dt.float8_e4m3fn_x4
+ALU = mybir.AluOpType
+ACT = mybir.ActivationFunctionType
+
+P = 128
+ROWS = 64
+PACK = 4
+HALF = N // 2
+NCALL = 128
+X_SPLIT = 160
+W_SPLIT = 80
+HH_SPLIT = 168
+
+
+def tile_rows_frowsoft_kernel(tc, x, w1, w2, tp, hs, wo2, ob, osc, out):
+    nc = tc.nc
+    with ExitStack() as ctx:
+        sb = ctx.enter_context(tc.tile_pool(name="sb", bufs=1))
+        ps = ctx.enter_context(tc.psum_pool(name="ps", bufs=1))
+        ctx.enter_context(tc.manual_schedule())
+
+        def tile(name, shape, dtype):
+            return sb.tile(shape, dtype, name=name, align_bytes=64)
+
+        def rows_of(g):
+            return slice(ROWS * g, ROWS * (g + 1))
+
+        def half(h):
+            return slice(HALF * h, HALF * (h + 1))
+
+        def by_partition(a):
+            return a.rearrange("g (q j) c -> (g q) j c", j=PACK)
+
+        def interleave(copy, dst, src, lo, hi):
+            copy(out=dst[:, lo * PACK:hi * PACK].rearrange("p (c i j) -> p c j i", i=4, j=PACK),
+                 in_=src[:, :, lo:hi].rearrange("p j (c i) -> p c j i", i=4))
+
+        def quantize(codes, scales, src):
+            nc.vector.quantize_mx(out=codes.bitcast(FP8X4), scales=scales, in_=src)
+
+        def product(dst, dst0, g, w_codes, w_scales, t, a_codes, a_scales, a0, width):
+            r = rows_of(g)
+            cols = slice(P * t, P * (t + 1))
+            for k in range(0, width, NCALL):
+                a = slice(a0 + k, a0 + k + NCALL)
+                nc.tensor.matmul_mx(out=dst[:, dst0 + k:dst0 + k + NCALL],
+                                    lhsT=w_codes[r, cols].bitcast(FP8X4), lhsT_scale=w_scales[r, cols],
+                                    rhs=a_codes[r, a].bitcast(FP8X4), rhs_scale=a_scales[r, a], start=True, stop=True)
+
+        x_raw = [tile("x_raw%d" % h, [P, PACK, HALF], F32) for h in range(2)]
+        w1_raw = tile("w1_raw", [P, PACK, M], F32)
+        w2_raw = tile("w2_raw", [P, PACK, M], F32)
+        wo_raw = tile("wo_raw", [P, PACK, O], F32)
+        tp_sb = tile("tp_sb", [P, G, 2], F32)
+        hs_sb = tile("hs_sb", [P, G, 2], F32)
+        ob_sb = tile("ob_sb", [P, G * 2], F32)
+        osc_sb = tile("osc_sb", [P, G * 2], F32)
+        for h in range(2):
+            nc.sync.dma_start(out=x_raw[h][:], in_=by_partition(x)[:, :, half(h)])
+        nc.sync.dma_start(out=w1_raw[:], in_=by_partition(w1))
+        nc.sync.dma_start(out=w2_raw[:], in_=by_partition(w2))
+        for dst, src in ((tp_sb, tp), (hs_sb, hs)):
+            nc.sync.dma_start(out=dst[:], in_=src.rearrange("g (p t) o -> p g (t o)", t=2))
+        nc.sync.dma_start(out=wo_raw[:], in_=by_partition(wo2))
+        with nc.allow_non_contiguous_dma(reason="one value a partition"):
+            nc.sync.dma_start(out=ob_sb[:], in_=ob.rearrange("g (t p) o -> p (g t o)", p=P))
+            nc.sync.dma_start(out=osc_sb[:], in_=osc.rearrange("g (t p) o -> p (g t o)", p=P))
+
+        x_bf = [tile("x_bf%d" % h, [P, HALF * PACK], BF16) for h in range(2)]
+        x_codes = tile("x_codes", [P, N], U32)
+        x_scales = tile("x_scales", [P, N], U8)
+        for h in range(2):
+            interleave(nc.vector.tensor_copy, x_bf[h], x_raw[h], 0, X_SPLIT)
+            interleave(nc.scalar.copy, x_bf[h], x_raw[h], X_SPLIT, HALF)
+            quantize(x_codes[:, half(h)], x_scales[:, half(h)], x_bf[h][:])
+
+        w1_bf = [tile("w1_bf%d" % t, [P, P * PACK], BF16) for t in range(2)]
+        w1_codes = tile("w1_codes", [P, M], U32)
+        w1_scales = tile("w1_scales", [P, M], U8)
+
+        def deal(copy, t, lo, hi):
+            copy(out=w1_bf[t][:, lo * PACK:hi * PACK].rearrange("p (c i j) -> p c j i", i=2, j=PACK),
+                 in_=w1_raw[:, :, 2 * lo:2 * hi].rearrange("p j (c i t) -> p t c j i", i=2, t=2)[:, t])
+
+        for t in range(2):
+            deal(nc.vector.tensor_copy, t, 0, W_SPLIT)
+            deal(nc.scalar.copy, t, W_SPLIT, P)
+        for t in range(2):
+            quantize(w1_codes[:, P * t:P * (t + 1)], w1_scales[:, P * t:P * (t + 1)], w1_bf[t][:])
+        bank_a = [[ps.tile([P, N], F32, name="bank_a%d%d" % (g, i)) for i in range(2)] for g in range(G)]
+        bank_b = [[ps.tile([P, N], F32, name="bank_b%d%d" % (g, i)) for i in range(2)] for g in range(G)]
+        for g in range(G):
+            for t in range(2):
+                product(bank_a[g][t], 0, g, w1_codes, w1_scales, t, x_codes, x_scales, 0, N)
+
+        w2_bf = tile("w2_bf", [P, M * PACK], BF16)
+        w2_codes = tile("w2_codes", [P, M], U32)
+        w2_scales = tile("w2_scales", [P, M], U8)
+        w2_dst = w2_bf[:].rearrange("p (t c i j) -> p c j i t", t=2, i=2, j=PACK)
+        w2_src = w2_raw[:].rearrange("p j (c i t) -> p c j i t", i=2, t=2)
+        nc.vector.tensor_copy(out=w2_dst[:, 0:W_SPLIT // 2], in_=w2_src[:, 0:W_SPLIT // 2])
+        nc.scalar.copy(out=w2_dst[:, W_SPLIT // 2:P // 2], in_=w2_src[:, W_SPLIT // 2:P // 2])
+        neg_tp = tile("neg_tp", [P, G, 2], F32)
+        nc.vector.tensor_scalar(out=neg_tp[:], in0=tp_sb[:], scalar1=-1.0, scalar2=None, op0=ALU.mult)
+        quantize(w2_codes[:], w2_scales[:], w2_bf[:])
+        for h in range(2):
+            for g in range(G):
+                for t in range(2):
+                    product(bank_b[g][h], HALF * t, g, w2_codes, w2_scales, t, x_codes, x_scales, HALF * h, HALF)
+
+        neg_s = [[tile("neg_s%d%d" % (g, t), [P, N], F32) for t in range(2)] for g in range(G)]
+        p1 = [[tile("p1_%d%d" % (g, t), [P, N], F32) for t in range(2)] for g in range(G)]
+        neg_max = [[tile("neg_max%d%d" % (g, t), [P, 1], F32) for t in range(2)] for g in range(G)]
+        zs = tile("zs", [P, 2 * G], F32)
+        inv_zs = tile("inv_zs", [P, 2 * G], F32)
+        factor = tile("factor", [P, 2 * G], F32)
+        hs_cols = hs_sb[:].rearrange("p g t -> p (g t)")
+        pairs = [[tile("pairs%d%d" % (g, h), [P, 2, HALF], BF16) for h in range(2)] for g in range(G)]
+        fours = [tile("fours%d" % h, [P, PACK, HALF], BF16) for h in range(2)]
+
+        def softmax_numerators(g, t):
+            nc.vector.tensor_scalar(out=neg_s[g][t][:], in0=bank_a[g][t][:], scalar1=neg_tp[:, g, t:t + 1], scalar2=None,
+                                    op0=ALU.mult, op1=ALU.min, accum_out=neg_max[g][t][:])
+            nc.scalar.activation(out=p1[g][t][:], in_=neg_s[g][t][:], func=ACT.Exp, bias=neg_max[g][t][:], scale=-1.0,
+                                 accum_out=zs[:, 2 * g + t:2 * g + t + 1])
+
+        def invert(lo, hi):
+            nc.vector.reciprocal(out=inv_zs[:, lo:hi], in_=zs[:, lo:hi])
+
+        def make_factor(lo, hi):
+            nc.vector.scalar_tensor_tensor(out=factor[:, lo:hi], in0=inv_zs[:, lo:hi], scalar=512.0,
+                                           in1=hs_cols[:, lo:hi], op0=ALU.mult, op1=ALU.mult)
+
+        def weigh(g, t, h):
+            nc.vector.scalar_tensor_tensor(out=pairs[g][h][:, t, :], in0=p1[g][t][:, half(h)],
+                                           scalar=factor[:, 2 * g + t:2 * g + t + 1], in1=bank_b[g][h][:, half(t)],
+                                           op0=ALU.mult, op1=ALU.mult)
+
+        def bring_home(g, h):
+            nc.sync.dma_start(out=fours[h][rows_of(g), :, :].rearrange("q (r t) n -> q r (t n)", r=2),
+                              in_=pairs[g][h][:].rearrange("p t n -> p (t n)"))
+
+        for g in range(G):
+            for t in range(2):
+                softmax_numerators(g, t)
+
+        wo_bf = tile("wo_bf", [P, O * PACK], BF16)
+        wo_codes = tile("wo_codes", [P, O], U32)
+        wo_scales = tile("wo_scales", [P, O], U8)
+        interleave(nc.scalar.copy, wo_bf, wo_raw, 0, O)
+
+        invert(0, 2)
+        invert(2, 3)
+        make_factor(0, 2)
+        make_factor(2, 3)
+        weigh(0, 0, 0)
+        invert(3, 4)
+        weigh(0, 1, 0)
+        bring_home(0, 0)
+        make_factor(3, 4)
+        weigh(1, 0, 0)
+        weigh(1, 1, 0)
+        bring_home(1, 0)
+        for g in range(G):
+            weigh(g, 0, 1)
+            weigh(g, 1, 1)
+            bring_home(g, 1)
+        quantize(wo_codes[:], wo_scales[:], wo_bf[:])
+
+        hh_bf = [tile("hh_bf%d" % h, [P, HALF * PACK], BF16) for h in range(2)]
+        hh_codes = [tile("hh_codes%d" % h, [P, HALF], U32) for h in range(2)]
+        hh_scales = [tile("hh_scales%d" % h, [P, HALF], U8) for h in range(2)]
+        th = [[[tile("th%d%d%d" % (g, t, h), [P, HALF], F32) for h in range(2)] for t in range(2)] for g in range(G)]
+        res = [[[tile("res%d%d%d" % (g, t, h), [P, HALF], F32) for h in range(2)] for t in range(2)] for g in range(G)]
+        y_banks = [bank_a, bank_b]
+
+        def second_products(h):
+            quantize(hh_codes[h][:], hh_scales[h][:], hh_bf[h][:])
+            for g in range(G):
+                for t in range(2):
+                    product(y_banks[h][g][t], 0, g, wo_codes, wo_scales, t, hh_codes[h], hh_scales[h], 0, HALF)
+
+        def squash(g, t, h):
+            c = 2 * g + t
+            nc.scalar.activation(out=th[g][t][h][:], in_=y_banks[h][g][t][:, 0:HALF], func=ACT.Tanh,
+                                 bias=ob_sb[:, c:c + 1], scale=1.0)
+
+        def finish(g, t, h):
+            c = 2 * g + t
+            nc.vector.tensor_scalar(out=res[g][t][h][:], in0=th[g][t][h][:], scalar1=osc_sb[:, c:c + 1], scalar2=None,
+                                    op0=ALU.mult)
+            nc.sync.dma_start(out=out[g, P * t:P * (t + 1), half(h)], in_=res[g][t][h][:])
+
+        interleave(nc.vector.tensor_copy, hh_bf[0], fours[0], 0, HH_SPLIT)
+        interleave(nc.scalar.copy, hh_bf[0], fours[0], HH_SPLIT, HALF)
+        second_products(0)
+        interleave(nc.vector.tensor_copy, hh_bf[1], fours[1], 0, HALF)
+        second_products(1)
+        for h in range(2):
+            for g in range(G):
+                for t in range(2):
+                    squash(g, t, h)
+                    finish(g, t, h)

@@ -18,9 +18,9 @@ ROWS = 64
 PACK = 4
 HALF = N // 2
 NCALL = 128
-X_SPLIT = 160
-W_SPLIT = 80
-HH_SPLIT = 168
+X_SPLIT = 168
+W_SPLIT = 84
+HH_SPLIT = 88
 
 
 def tile_rows_frowsoft_kernel(tc, x, w1, w2, tp, hs, wo2, ob, osc, out):
@@ -70,9 +70,9 @@ def tile_rows_frowsoft_kernel(tc, x, w1, w2, tp, hs, wo2, ob, osc, out):
             nc.sync.dma_start(out=x_raw[h][:], in_=by_partition(x)[:, :, half(h)])
         nc.sync.dma_start(out=w1_raw[:], in_=by_partition(w1))
         nc.sync.dma_start(out=w2_raw[:], in_=by_partition(w2))
-        for dst, src in ((tp_sb, tp), (hs_sb, hs)):
-            nc.sync.dma_start(out=dst[:], in_=src.rearrange("g (p t) o -> p g (t o)", t=2))
+        nc.scalar.dma_start(out=tp_sb[:], in_=tp.rearrange("g (p t) o -> p g (t o)", t=2))
         nc.sync.dma_start(out=wo_raw[:], in_=by_partition(wo2))
+        nc.sync.dma_start(out=hs_sb[:], in_=hs.rearrange("g (p t) o -> p g (t o)", t=2))
         with nc.allow_non_contiguous_dma(reason="one value a partition"):
             nc.sync.dma_start(out=ob_sb[:], in_=ob.rearrange("g (t p) o -> p (g t o)", p=P))
             nc.sync.dma_start(out=osc_sb[:], in_=osc.rearrange("g (t p) o -> p (g t o)", p=P))
@@ -80,44 +80,38 @@ def tile_rows_frowsoft_kernel(tc, x, w1, w2, tp, hs, wo2, ob, osc, out):
         x_bf = [tile("x_bf%d" % h, [P, HALF * PACK], BF16) for h in range(2)]
         x_codes = tile("x_codes", [P, N], U32)
         x_scales = tile("x_scales", [P, N], U8)
+        neg_tp = tile("neg_tp", [P, G, 2], F32)
         for h in range(2):
             interleave(nc.vector.tensor_copy, x_bf[h], x_raw[h], 0, X_SPLIT)
             interleave(nc.scalar.copy, x_bf[h], x_raw[h], X_SPLIT, HALF)
             quantize(x_codes[:, half(h)], x_scales[:, half(h)], x_bf[h][:])
 
-        w1_bf = [tile("w1_bf%d" % t, [P, P * PACK], BF16) for t in range(2)]
-        w1_codes = tile("w1_codes", [P, M], U32)
-        w1_scales = tile("w1_scales", [P, M], U8)
+        def first_layer_weights(name, raw):
+            w_bf = [tile("%s_bf%d" % (name, t), [P, P * PACK], BF16) for t in range(2)]
+            codes = tile(name + "_codes", [P, M], U32)
+            scales = tile(name + "_scales", [P, M], U8)
+            for t in range(2):
+                for copy, lo, hi in ((nc.vector.tensor_copy, 0, W_SPLIT), (nc.scalar.copy, W_SPLIT, P)):
+                    copy(out=w_bf[t][:, lo * PACK:hi * PACK].rearrange("p (c i j) -> p c j i", i=2, j=PACK),
+                         in_=raw[:, :, 2 * lo:2 * hi].rearrange("p j (c i t) -> p t c j i", i=2, t=2)[:, t])
+            for t in range(2):
+                quantize(codes[:, P * t:P * (t + 1)], scales[:, P * t:P * (t + 1)], w_bf[t][:])
+            return codes, scales
 
-        def deal(copy, t, lo, hi):
-            copy(out=w1_bf[t][:, lo * PACK:hi * PACK].rearrange("p (c i j) -> p c j i", i=2, j=PACK),
-                 in_=w1_raw[:, :, 2 * lo:2 * hi].rearrange("p j (c i t) -> p t c j i", i=2, t=2)[:, t])
-
-        for t in range(2):
-            deal(nc.vector.tensor_copy, t, 0, W_SPLIT)
-            deal(nc.scalar.copy, t, W_SPLIT, P)
-        for t in range(2):
-            quantize(w1_codes[:, P * t:P * (t + 1)], w1_scales[:, P * t:P * (t + 1)], w1_bf[t][:])
         bank_a = [[ps.tile([P, N], F32, name="bank_a%d%d" % (g, i)) for i in range(2)] for g in range(G)]
         bank_b = [[ps.tile([P, N], F32, name="bank_b%d%d" % (g, i)) for i in range(2)] for g in range(G)]
+        w1_codes, w1_scales = first_layer_weights("w1", w1_raw)
         for g in range(G):
             for t in range(2):
                 product(bank_a[g][t], 0, g, w1_codes, w1_scales, t, x_codes, x_scales, 0, N)
-
-        w2_bf = tile("w2_bf", [P, M * PACK], BF16)
-        w2_codes = tile("w2_codes", [P, M], U32)
-        w2_scales = tile("w2_scales", [P, M], U8)
-        w2_dst = w2_bf[:].rearrange("p (t c i j) -> p c j i t", t=2, i=2, j=PACK)
-        w2_src = w2_raw[:].rearrange("p j (c i t) -> p c j i t", i=2, t=2)
-        nc.vector.tensor_copy(out=w2_dst[:, 0:W_SPLIT // 2], in_=w2_src[:, 0:W_SPLIT // 2])
-        nc.scalar.copy(out=w2_dst[:, W_SPLIT // 2:P // 2], in_=w2_src[:, W_SPLIT // 2:P // 2])
-        neg_tp = tile("neg_tp", [P, G, 2], F32)
         nc.vector.tensor_scalar(out=neg_tp[:], in0=tp_sb[:], scalar1=-1.0, scalar2=None, op0=ALU.mult)
-        quantize(w2_codes[:], w2_scales[:], w2_bf[:])
+        w2_codes, w2_scales = first_layer_weights("w2", w2_raw)
         for h in range(2):
-            for g in range(G):
-                for t in range(2):
-                    product(bank_b[g][h], HALF * t, g, w2_codes, w2_scales, t, x_codes, x_scales, HALF * h, HALF)
+            for t in range(2):
+                for k in range(0, HALF, NCALL):
+                    for g in range(G):
+                        product(bank_b[g][h], HALF * t + k, g, w2_codes, w2_scales, t, x_codes, x_scales,
+                                HALF * h + k, NCALL)
 
         neg_s = [[tile("neg_s%d%d" % (g, t), [P, N], F32) for t in range(2)] for g in range(G)]
         p1 = [[tile("p1_%d%d" % (g, t), [P, N], F32) for t in range(2)] for g in range(G)]
@@ -126,8 +120,8 @@ def tile_rows_frowsoft_kernel(tc, x, w1, w2, tp, hs, wo2, ob, osc, out):
         inv_zs = tile("inv_zs", [P, 2 * G], F32)
         factor = tile("factor", [P, 2 * G], F32)
         hs_cols = hs_sb[:].rearrange("p g t -> p (g t)")
-        pairs = [[tile("pairs%d%d" % (g, h), [P, 2, HALF], BF16) for h in range(2)] for g in range(G)]
-        fours = [tile("fours%d" % h, [P, PACK, HALF], BF16) for h in range(2)]
+        pairs = [[tile("pairs%d%d" % (g, h), [P, 2, 2, NCALL], BF16) for h in range(2)] for g in range(G)]
+        fours = [tile("fours%d" % k, [P, PACK, NCALL], BF16) for k in range(4)]
 
         def softmax_numerators(g, t):
             nc.vector.tensor_scalar(out=neg_s[g][t][:], in0=bank_a[g][t][:], scalar1=neg_tp[:, g, t:t + 1], scalar2=None,
@@ -142,14 +136,19 @@ def tile_rows_frowsoft_kernel(tc, x, w1, w2, tp, hs, wo2, ob, osc, out):
             nc.vector.scalar_tensor_tensor(out=factor[:, lo:hi], in0=inv_zs[:, lo:hi], scalar=512.0,
                                            in1=hs_cols[:, lo:hi], op0=ALU.mult, op1=ALU.mult)
 
-        def weigh(g, t, h):
-            nc.vector.scalar_tensor_tensor(out=pairs[g][h][:, t, :], in0=p1[g][t][:, half(h)],
-                                           scalar=factor[:, 2 * g + t:2 * g + t + 1], in1=bank_b[g][h][:, half(t)],
-                                           op0=ALU.mult, op1=ALU.mult)
+        def weigh(g, t, k0, k1):
+            h = k0 // 2
+            lo, hi = NCALL * k0, NCALL * k1
+            nc.vector.scalar_tensor_tensor(
+                out=pairs[g][h][:, k0 - 2 * h:k1 - 2 * h, t, :],
+                in0=p1[g][t][:, lo:hi].rearrange("p (k n) -> p k n", n=NCALL),
+                scalar=factor[:, 2 * g + t:2 * g + t + 1],
+                in1=bank_b[g][h][:, HALF * (t - h) + lo:HALF * (t - h) + hi].rearrange("p (k n) -> p k n", n=NCALL),
+                op0=ALU.mult, op1=ALU.mult)
 
-        def bring_home(g, h):
-            nc.sync.dma_start(out=fours[h][rows_of(g), :, :].rearrange("q (r t) n -> q r (t n)", r=2),
-                              in_=pairs[g][h][:].rearrange("p t n -> p (t n)"))
+        def bring_home(g, k):
+            nc.sync.dma_start(out=fours[k][rows_of(g), :, :].rearrange("q (r t) n -> q r (t n)", r=2),
+                              in_=pairs[g][k // 2][:, k % 2].rearrange("p t n -> p (t n)"))
 
         for g in range(G):
             for t in range(2):
@@ -164,51 +163,81 @@ def tile_rows_frowsoft_kernel(tc, x, w1, w2, tp, hs, wo2, ob, osc, out):
         invert(2, 3)
         make_factor(0, 2)
         make_factor(2, 3)
-        weigh(0, 0, 0)
+        weigh(0, 0, 0, 2)
         invert(3, 4)
-        weigh(0, 1, 0)
+        weigh(0, 1, 0, 2)
         bring_home(0, 0)
+        bring_home(0, 1)
         make_factor(3, 4)
-        weigh(1, 0, 0)
-        weigh(1, 1, 0)
-        bring_home(1, 0)
-        for g in range(G):
-            weigh(g, 0, 1)
-            weigh(g, 1, 1)
-            bring_home(g, 1)
+        weigh(1, 0, 0, 2)
+        for k in range(2):
+            weigh(1, 1, k, k + 1)
+            bring_home(1, k)
+        weigh(0, 0, 2, 4)
+        weigh(0, 1, 2, 4)
+        bring_home(0, 2)
+        bring_home(0, 3)
+        weigh(1, 0, 2, 4)
+        for k in range(2, 4):
+            weigh(1, 1, k, k + 1)
+            bring_home(1, k)
         quantize(wo_codes[:], wo_scales[:], wo_bf[:])
 
-        hh_bf = [tile("hh_bf%d" % h, [P, HALF * PACK], BF16) for h in range(2)]
-        hh_codes = [tile("hh_codes%d" % h, [P, HALF], U32) for h in range(2)]
-        hh_scales = [tile("hh_scales%d" % h, [P, HALF], U8) for h in range(2)]
-        th = [[[tile("th%d%d%d" % (g, t, h), [P, HALF], F32) for h in range(2)] for t in range(2)] for g in range(G)]
-        res = [[[tile("res%d%d%d" % (g, t, h), [P, HALF], F32) for h in range(2)] for t in range(2)] for g in range(G)]
-        y_banks = [bank_a, bank_b]
+        hh_bf = [tile("hh_bf%d" % k, [P, NCALL * PACK], BF16) for k in range(4)]
+        hh_codes = [tile("hh_codes%d" % k, [P, NCALL], U32) for k in range(4)]
+        hh_scales = [tile("hh_scales%d" % k, [P, NCALL], U8) for k in range(4)]
+        widths = [NCALL, NCALL, HALF]
+        th = [[[tile("th%d%d%d" % (g, t, c), [P, widths[c]], F32) for c in range(3)] for t in range(2)] for g in range(G)]
+        res = [[tile("res%d%d" % (g, c), [P, 2, widths[c]], F32) for c in range(3)] for g in range(G)]
+        y_place = [(bank_a, 0), (bank_b, 0), (bank_a, NCALL), (bank_a, 2 * NCALL)]
 
-        def second_products(h):
-            quantize(hh_codes[h][:], hh_scales[h][:], hh_bf[h][:])
+        def hh_words(k, shared):
+            if shared:
+                interleave(nc.vector.tensor_copy, hh_bf[k], fours[k], 0, HH_SPLIT)
+                interleave(nc.scalar.copy, hh_bf[k], fours[k], HH_SPLIT, NCALL)
+            else:
+                interleave(nc.vector.tensor_copy, hh_bf[k], fours[k], 0, NCALL)
+
+        def second_product(t, k):
+            banks, col = y_place[k]
             for g in range(G):
-                for t in range(2):
-                    product(y_banks[h][g][t], 0, g, wo_codes, wo_scales, t, hh_codes[h], hh_scales[h], 0, HALF)
+                product(banks[g][t], col, g, wo_codes, wo_scales, t, hh_codes[k], hh_scales[k], 0, NCALL)
 
-        def squash(g, t, h):
-            c = 2 * g + t
-            nc.scalar.activation(out=th[g][t][h][:], in_=y_banks[h][g][t][:, 0:HALF], func=ACT.Tanh,
-                                 bias=ob_sb[:, c:c + 1], scale=1.0)
+        def squash(c):
+            banks, col = y_place[c]
+            for t in range(2):
+                for g in range(G):
+                    nc.scalar.activation(out=th[g][t][c][:], in_=banks[g][t][:, col:col + widths[c]], func=ACT.Tanh,
+                                         bias=ob_sb[:, 2 * g + t:2 * g + t + 1], scale=1.0)
 
-        def finish(g, t, h):
-            c = 2 * g + t
-            nc.vector.tensor_scalar(out=res[g][t][h][:], in0=th[g][t][h][:], scalar1=osc_sb[:, c:c + 1], scalar2=None,
-                                    op0=ALU.mult)
-            nc.sync.dma_start(out=out[g, P * t:P * (t + 1), half(h)], in_=res[g][t][h][:])
+        def finish(c):
+            lo = NCALL * c
+            for t in range(2):
+                for g in range(G):
+                    nc.vector.tensor_scalar(out=res[g][c][:, t, :], in0=th[g][t][c][:],
+                                            scalar1=osc_sb[:, 2 * g + t:2 * g + t + 1], scalar2=None, op0=ALU.mult)
+                    if c == 2:
+                        nc.sync.dma_start(out=out[g, P * t:P * (t + 1), lo:N], in_=res[g][c][:, t, :])
+                    elif t == 1:
+                        nc.sync.dma_start(out=out[g, :, lo:lo + NCALL].rearrange("(t p) n -> p t n", p=P),
+                                          in_=res[g][c][:])
 
-        interleave(nc.vector.tensor_copy, hh_bf[0], fours[0], 0, HH_SPLIT)
-        interleave(nc.scalar.copy, hh_bf[0], fours[0], HH_SPLIT, HALF)
-        second_products(0)
-        interleave(nc.vector.tensor_copy, hh_bf[1], fours[1], 0, HALF)
-        second_products(1)
-        for h in range(2):
-            for g in range(G):
-                for t in range(2):
-                    squash(g, t, h)
-                    finish(g, t, h)
+        hh_words(0, True)
+        hh_words(1, True)
+        for k in range(2):
+            quantize(hh_codes[k][:], hh_scales[k][:], hh_bf[k][:])
+            for t in range(2):
+                second_product(t, k)
+        hh_words(2, True)
+        hh_words(3, False)
+        squash(0)
+        squash(1)
+        quantize(hh_codes[2][:], hh_scales[2][:], hh_bf[2][:])
+        second_product(0, 2)
+        quantize(hh_codes[3][:], hh_scales[3][:], hh_bf[3][:])
+        second_product(0, 3)
+        second_product(1, 2)
+        second_product(1, 3)
+        squash(2)
+        for c in range(3):
+            finish(c)

@@ -18,7 +18,7 @@ ROWS = 64
 PACK = 4
 HALF = N // 2
 NCALL = 128
-X_SPLIT = 168
+X_SPLIT = 40
 W_SPLIT = 84
 HH_SPLIT = 88
 
@@ -58,7 +58,7 @@ def tile_rows_frowsoft_kernel(tc, x, w1, w2, tp, hs, wo2, ob, osc, out):
                                     lhsT=w_codes[r, cols].bitcast(FP8X4), lhsT_scale=w_scales[r, cols],
                                     rhs=a_codes[r, a].bitcast(FP8X4), rhs_scale=a_scales[r, a], start=True, stop=True)
 
-        x_raw = [tile("x_raw%d" % h, [P, PACK, HALF], F32) for h in range(2)]
+        x_raw = tile("x_raw", [P, PACK, N], F32)
         w1_raw = tile("w1_raw", [P, PACK, M], F32)
         w2_raw = tile("w2_raw", [P, PACK, M], F32)
         wo_raw = tile("wo_raw", [P, PACK, O], F32)
@@ -66,8 +66,7 @@ def tile_rows_frowsoft_kernel(tc, x, w1, w2, tp, hs, wo2, ob, osc, out):
         hs_sb = tile("hs_sb", [P, G, 2], F32)
         ob_sb = tile("ob_sb", [P, G * 2], F32)
         osc_sb = tile("osc_sb", [P, G * 2], F32)
-        for h in range(2):
-            nc.sync.dma_start(out=x_raw[h][:], in_=by_partition(x)[:, :, half(h)])
+        nc.sync.dma_start(out=x_raw[:], in_=by_partition(x))
         nc.sync.dma_start(out=w1_raw[:], in_=by_partition(w1))
         nc.sync.dma_start(out=w2_raw[:], in_=by_partition(w2))
         nc.scalar.dma_start(out=tp_sb[:], in_=tp.rearrange("g (p t) o -> p g (t o)", t=2))
@@ -81,17 +80,18 @@ def tile_rows_frowsoft_kernel(tc, x, w1, w2, tp, hs, wo2, ob, osc, out):
         x_codes = tile("x_codes", [P, N], U32)
         x_scales = tile("x_scales", [P, N], U8)
         neg_tp = tile("neg_tp", [P, G, 2], F32)
+        interleave(nc.vector.tensor_copy, x_bf[0], x_raw[:, :, half(0)], 0, HALF)
+        interleave(nc.vector.tensor_copy, x_bf[1], x_raw[:, :, half(1)], 0, X_SPLIT)
+        interleave(nc.scalar.copy, x_bf[1], x_raw[:, :, half(1)], X_SPLIT, HALF)
         for h in range(2):
-            interleave(nc.vector.tensor_copy, x_bf[h], x_raw[h], 0, X_SPLIT)
-            interleave(nc.scalar.copy, x_bf[h], x_raw[h], X_SPLIT, HALF)
             quantize(x_codes[:, half(h)], x_scales[:, half(h)], x_bf[h][:])
 
-        def first_layer_weights(name, raw):
+        def first_layer_weights(name, raw, splits):
             w_bf = [tile("%s_bf%d" % (name, t), [P, P * PACK], BF16) for t in range(2)]
             codes = tile(name + "_codes", [P, M], U32)
             scales = tile(name + "_scales", [P, M], U8)
             for t in range(2):
-                for copy, lo, hi in ((nc.vector.tensor_copy, 0, W_SPLIT), (nc.scalar.copy, W_SPLIT, P)):
+                for copy, lo, hi in ((nc.vector.tensor_copy, 0, splits[t]), (nc.scalar.copy, splits[t], P)):
                     copy(out=w_bf[t][:, lo * PACK:hi * PACK].rearrange("p (c i j) -> p c j i", i=2, j=PACK),
                          in_=raw[:, :, 2 * lo:2 * hi].rearrange("p j (c i t) -> p t c j i", i=2, t=2)[:, t])
             for t in range(2):
@@ -100,12 +100,12 @@ def tile_rows_frowsoft_kernel(tc, x, w1, w2, tp, hs, wo2, ob, osc, out):
 
         bank_a = [[ps.tile([P, N], F32, name="bank_a%d%d" % (g, i)) for i in range(2)] for g in range(G)]
         bank_b = [[ps.tile([P, N], F32, name="bank_b%d%d" % (g, i)) for i in range(2)] for g in range(G)]
-        w1_codes, w1_scales = first_layer_weights("w1", w1_raw)
+        w1_codes, w1_scales = first_layer_weights("w1", w1_raw, (P - W_SPLIT, W_SPLIT))
         for g in range(G):
             for t in range(2):
                 product(bank_a[g][t], 0, g, w1_codes, w1_scales, t, x_codes, x_scales, 0, N)
         nc.vector.tensor_scalar(out=neg_tp[:], in0=tp_sb[:], scalar1=-1.0, scalar2=None, op0=ALU.mult)
-        w2_codes, w2_scales = first_layer_weights("w2", w2_raw)
+        w2_codes, w2_scales = first_layer_weights("w2", w2_raw, (W_SPLIT, W_SPLIT))
         for h in range(2):
             for t in range(2):
                 for k in range(0, HALF, NCALL):
@@ -186,9 +186,8 @@ def tile_rows_frowsoft_kernel(tc, x, w1, w2, tp, hs, wo2, ob, osc, out):
         hh_bf = [tile("hh_bf%d" % k, [P, NCALL * PACK], BF16) for k in range(4)]
         hh_codes = [tile("hh_codes%d" % k, [P, NCALL], U32) for k in range(4)]
         hh_scales = [tile("hh_scales%d" % k, [P, NCALL], U8) for k in range(4)]
-        widths = [NCALL, NCALL, HALF]
-        th = [[[tile("th%d%d%d" % (g, t, c), [P, widths[c]], F32) for c in range(3)] for t in range(2)] for g in range(G)]
-        res = [[tile("res%d%d" % (g, c), [P, 2, widths[c]], F32) for c in range(3)] for g in range(G)]
+        th = [[[tile("th%d%d%d" % (g, t, h), [P, HALF], F32) for h in range(2)] for t in range(2)] for g in range(G)]
+        res = [[[tile("res%d%d%d" % (g, t, h), [P, HALF], F32) for h in range(2)] for t in range(2)] for g in range(G)]
         y_place = [(bank_a, 0), (bank_b, 0), (bank_a, NCALL), (bank_a, 2 * NCALL)]
 
         def hh_words(k, shared):
@@ -203,24 +202,21 @@ def tile_rows_frowsoft_kernel(tc, x, w1, w2, tp, hs, wo2, ob, osc, out):
             for g in range(G):
                 product(banks[g][t], col, g, wo_codes, wo_scales, t, hh_codes[k], hh_scales[k], 0, NCALL)
 
-        def squash(c):
-            banks, col = y_place[c]
+        def squash(k0, k1):
+            banks, col = y_place[k0]
+            width = NCALL * (k1 - k0)
+            lo = NCALL * (k0 % 2)
             for t in range(2):
                 for g in range(G):
-                    nc.scalar.activation(out=th[g][t][c][:], in_=banks[g][t][:, col:col + widths[c]], func=ACT.Tanh,
-                                         bias=ob_sb[:, 2 * g + t:2 * g + t + 1], scale=1.0)
+                    nc.scalar.activation(out=th[g][t][k0 // 2][:, lo:lo + width], in_=banks[g][t][:, col:col + width],
+                                         func=ACT.Tanh, bias=ob_sb[:, 2 * g + t:2 * g + t + 1], scale=1.0)
 
-        def finish(c):
-            lo = NCALL * c
+        def finish(h):
             for t in range(2):
                 for g in range(G):
-                    nc.vector.tensor_scalar(out=res[g][c][:, t, :], in0=th[g][t][c][:],
+                    nc.vector.tensor_scalar(out=res[g][t][h][:], in0=th[g][t][h][:],
                                             scalar1=osc_sb[:, 2 * g + t:2 * g + t + 1], scalar2=None, op0=ALU.mult)
-                    if c == 2:
-                        nc.sync.dma_start(out=out[g, P * t:P * (t + 1), lo:N], in_=res[g][c][:, t, :])
-                    elif t == 1:
-                        nc.sync.dma_start(out=out[g, :, lo:lo + NCALL].rearrange("(t p) n -> p t n", p=P),
-                                          in_=res[g][c][:])
+                    nc.sync.dma_start(out=out[g, P * t:P * (t + 1), half(h)], in_=res[g][t][h][:])
 
         hh_words(0, True)
         hh_words(1, True)
@@ -230,14 +226,14 @@ def tile_rows_frowsoft_kernel(tc, x, w1, w2, tp, hs, wo2, ob, osc, out):
                 second_product(t, k)
         hh_words(2, True)
         hh_words(3, False)
-        squash(0)
-        squash(1)
+        squash(0, 1)
+        squash(1, 2)
         quantize(hh_codes[2][:], hh_scales[2][:], hh_bf[2][:])
         second_product(0, 2)
         quantize(hh_codes[3][:], hh_scales[3][:], hh_bf[3][:])
         second_product(0, 3)
         second_product(1, 2)
         second_product(1, 3)
-        squash(2)
-        for c in range(3):
-            finish(c)
+        squash(2, 4)
+        for h in range(2):
+            finish(h)

from contextlib import ExitStack

import concourse.mybir as mybir

G, D, M, O, N = 2, 256, 256, 256, 512
FLOPS = 2 * G * N * (2 * D * M + M * O)

F32 = mybir.dt.float32
BF16 = mybir.dt.bfloat16
U32 = mybir.dt.uint32
U8 = mybir.dt.uint8
FP8X4 = mybir.dt.float8_e4m3fn_x4
ALU = mybir.AluOpType
ACT = mybir.ActivationFunctionType

P = 128
ROWS = 64
PACK = 4
HALF = N // 2
NCALL = 128
X_SPLIT = 40
W_SPLIT = 84
HH_SPLIT = 88


def tile_rows_frowsoft_kernel(tc, x, w1, w2, tp, hs, wo2, ob, osc, out):
    nc = tc.nc
    with ExitStack() as ctx:
        sb = ctx.enter_context(tc.tile_pool(name="sb", bufs=1))
        ps = ctx.enter_context(tc.psum_pool(name="ps", bufs=1))
        ctx.enter_context(tc.manual_schedule())

        def tile(name, shape, dtype):
            return sb.tile(shape, dtype, name=name, align_bytes=64)

        def rows_of(g):
            return slice(ROWS * g, ROWS * (g + 1))

        def half(h):
            return slice(HALF * h, HALF * (h + 1))

        def by_partition(a):
            return a.rearrange("g (q j) c -> (g q) j c", j=PACK)

        def interleave(copy, dst, src, lo, hi):
            copy(out=dst[:, lo * PACK:hi * PACK].rearrange("p (c i j) -> p c j i", i=4, j=PACK),
                 in_=src[:, :, lo:hi].rearrange("p j (c i) -> p c j i", i=4))

        def quantize(codes, scales, src):
            nc.vector.quantize_mx(out=codes.bitcast(FP8X4), scales=scales, in_=src)

        def product(dst, dst0, g, w_codes, w_scales, t, a_codes, a_scales, a0, width):
            r = rows_of(g)
            cols = slice(P * t, P * (t + 1))
            for k in range(0, width, NCALL):
                a = slice(a0 + k, a0 + k + NCALL)
                nc.tensor.matmul_mx(out=dst[:, dst0 + k:dst0 + k + NCALL],
                                    lhsT=w_codes[r, cols].bitcast(FP8X4), lhsT_scale=w_scales[r, cols],
                                    rhs=a_codes[r, a].bitcast(FP8X4), rhs_scale=a_scales[r, a], start=True, stop=True)

        x_raw = tile("x_raw", [P, PACK, N], F32)
        w1_raw = tile("w1_raw", [P, PACK, M], F32)
        w2_raw = tile("w2_raw", [P, PACK, M], F32)
        wo_raw = tile("wo_raw", [P, PACK, O], F32)
        tp_sb = tile("tp_sb", [P, G, 2], F32)
        hs_sb = tile("hs_sb", [P, G, 2], F32)
        ob_sb = tile("ob_sb", [P, G * 2], F32)
        osc_sb = tile("osc_sb", [P, G * 2], F32)
        nc.sync.dma_start(out=x_raw[:], in_=by_partition(x))
        nc.sync.dma_start(out=w1_raw[:], in_=by_partition(w1))
        nc.sync.dma_start(out=w2_raw[:], in_=by_partition(w2))
        nc.scalar.dma_start(out=tp_sb[:], in_=tp.rearrange("g (p t) o -> p g (t o)", t=2))
        nc.sync.dma_start(out=wo_raw[:], in_=by_partition(wo2))
        nc.sync.dma_start(out=hs_sb[:], in_=hs.rearrange("g (p t) o -> p g (t o)", t=2))
        with nc.allow_non_contiguous_dma(reason="one value a partition"):
            nc.sync.dma_start(out=ob_sb[:], in_=ob.rearrange("g (t p) o -> p (g t o)", p=P))
            nc.sync.dma_start(out=osc_sb[:], in_=osc.rearrange("g (t p) o -> p (g t o)", p=P))

        x_bf = [tile("x_bf%d" % h, [P, HALF * PACK], BF16) for h in range(2)]
        x_codes = tile("x_codes", [P, N], U32)
        x_scales = tile("x_scales", [P, N], U8)
        neg_tp = tile("neg_tp", [P, G, 2], F32)
        interleave(nc.vector.tensor_copy, x_bf[0], x_raw[:, :, half(0)], 0, HALF)
        interleave(nc.vector.tensor_copy, x_bf[1], x_raw[:, :, half(1)], 0, X_SPLIT)
        interleave(nc.scalar.copy, x_bf[1], x_raw[:, :, half(1)], X_SPLIT, HALF)
        for h in range(2):
            quantize(x_codes[:, half(h)], x_scales[:, half(h)], x_bf[h][:])

        def first_layer_weights(name, raw, splits):
            w_bf = [tile("%s_bf%d" % (name, t), [P, P * PACK], BF16) for t in range(2)]
            codes = tile(name + "_codes", [P, M], U32)
            scales = tile(name + "_scales", [P, M], U8)
            for t in range(2):
                for copy, lo, hi in ((nc.vector.tensor_copy, 0, splits[t]), (nc.scalar.copy, splits[t], P)):
                    copy(out=w_bf[t][:, lo * PACK:hi * PACK].rearrange("p (c i j) -> p c j i", i=2, j=PACK),
                         in_=raw[:, :, 2 * lo:2 * hi].rearrange("p j (c i t) -> p t c j i", i=2, t=2)[:, t])
            for t in range(2):
                quantize(codes[:, P * t:P * (t + 1)], scales[:, P * t:P * (t + 1)], w_bf[t][:])
            return codes, scales

        bank_a = [[ps.tile([P, N], F32, name="bank_a%d%d" % (g, i)) for i in range(2)] for g in range(G)]
        bank_b = [[ps.tile([P, N], F32, name="bank_b%d%d" % (g, i)) for i in range(2)] for g in range(G)]
        w1_codes, w1_scales = first_layer_weights("w1", w1_raw, (P - W_SPLIT, W_SPLIT))
        for g in range(G):
            for t in range(2):
                product(bank_a[g][t], 0, g, w1_codes, w1_scales, t, x_codes, x_scales, 0, N)
        nc.vector.tensor_scalar(out=neg_tp[:], in0=tp_sb[:], scalar1=-1.0, scalar2=None, op0=ALU.mult)
        w2_codes, w2_scales = first_layer_weights("w2", w2_raw, (W_SPLIT, W_SPLIT))
        for h in range(2):
            for t in range(2):
                for k in range(0, HALF, NCALL):
                    for g in range(G):
                        product(bank_b[g][h], HALF * t + k, g, w2_codes, w2_scales, t, x_codes, x_scales,
                                HALF * h + k, NCALL)

        neg_s = [[tile("neg_s%d%d" % (g, t), [P, N], F32) for t in range(2)] for g in range(G)]
        p1 = [[tile("p1_%d%d" % (g, t), [P, N], F32) for t in range(2)] for g in range(G)]
        neg_max = [[tile("neg_max%d%d" % (g, t), [P, 1], F32) for t in range(2)] for g in range(G)]
        zs = tile("zs", [P, 2 * G], F32)
        inv_zs = tile("inv_zs", [P, 2 * G], F32)
        factor = tile("factor", [P, 2 * G], F32)
        hs_cols = hs_sb[:].rearrange("p g t -> p (g t)")
        pairs = [[tile("pairs%d%d" % (g, h), [P, 2, 2, NCALL], BF16) for h in range(2)] for g in range(G)]
        fours = [tile("fours%d" % k, [P, PACK, NCALL], BF16) for k in range(4)]

        def softmax_numerators(g, t):
            nc.vector.tensor_scalar(out=neg_s[g][t][:], in0=bank_a[g][t][:], scalar1=neg_tp[:, g, t:t + 1], scalar2=None,
                                    op0=ALU.mult, op1=ALU.min, accum_out=neg_max[g][t][:])
            nc.scalar.activation(out=p1[g][t][:], in_=neg_s[g][t][:], func=ACT.Exp, bias=neg_max[g][t][:], scale=-1.0,
                                 accum_out=zs[:, 2 * g + t:2 * g + t + 1])

        def invert(lo, hi):
            nc.vector.reciprocal(out=inv_zs[:, lo:hi], in_=zs[:, lo:hi])

        def make_factor(lo, hi):
            nc.vector.scalar_tensor_tensor(out=factor[:, lo:hi], in0=inv_zs[:, lo:hi], scalar=512.0,
                                           in1=hs_cols[:, lo:hi], op0=ALU.mult, op1=ALU.mult)

        def weigh(g, t, k0, k1):
            h = k0 // 2
            lo, hi = NCALL * k0, NCALL * k1
            nc.vector.scalar_tensor_tensor(
                out=pairs[g][h][:, k0 - 2 * h:k1 - 2 * h, t, :],
                in0=p1[g][t][:, lo:hi].rearrange("p (k n) -> p k n", n=NCALL),
                scalar=factor[:, 2 * g + t:2 * g + t + 1],
                in1=bank_b[g][h][:, HALF * (t - h) + lo:HALF * (t - h) + hi].rearrange("p (k n) -> p k n", n=NCALL),
                op0=ALU.mult, op1=ALU.mult)

        def bring_home(g, k):
            nc.sync.dma_start(out=fours[k][rows_of(g), :, :].rearrange("q (r t) n -> q r (t n)", r=2),
                              in_=pairs[g][k // 2][:, k % 2].rearrange("p t n -> p (t n)"))

        for g in range(G):
            for t in range(2):
                softmax_numerators(g, t)

        wo_bf = tile("wo_bf", [P, O * PACK], BF16)
        wo_codes = tile("wo_codes", [P, O], U32)
        wo_scales = tile("wo_scales", [P, O], U8)
        interleave(nc.scalar.copy, wo_bf, wo_raw, 0, O)

        invert(0, 2)
        invert(2, 3)
        make_factor(0, 2)
        make_factor(2, 3)
        weigh(0, 0, 0, 2)
        invert(3, 4)
        weigh(0, 1, 0, 2)
        bring_home(0, 0)
        bring_home(0, 1)
        make_factor(3, 4)
        weigh(1, 0, 0, 2)
        for k in range(2):
            weigh(1, 1, k, k + 1)
            bring_home(1, k)
        weigh(0, 0, 2, 4)
        weigh(0, 1, 2, 4)
        bring_home(0, 2)
        bring_home(0, 3)
        weigh(1, 0, 2, 4)
        for k in range(2, 4):
            weigh(1, 1, k, k + 1)
            bring_home(1, k)
        quantize(wo_codes[:], wo_scales[:], wo_bf[:])

        hh_bf = [tile("hh_bf%d" % k, [P, NCALL * PACK], BF16) for k in range(4)]
        hh_codes = [tile("hh_codes%d" % k, [P, NCALL], U32) for k in range(4)]
        hh_scales = [tile("hh_scales%d" % k, [P, NCALL], U8) for k in range(4)]
        th = [[[tile("th%d%d%d" % (g, t, h), [P, HALF], F32) for h in range(2)] for t in range(2)] for g in range(G)]
        res = [[[tile("res%d%d%d" % (g, t, h), [P, HALF], F32) for h in range(2)] for t in range(2)] for g in range(G)]
        y_place = [(bank_a, 0), (bank_b, 0), (bank_a, NCALL), (bank_a, 2 * NCALL)]

        def hh_words(k, shared):
            if shared:
                interleave(nc.vector.tensor_copy, hh_bf[k], fours[k], 0, HH_SPLIT)
                interleave(nc.scalar.copy, hh_bf[k], fours[k], HH_SPLIT, NCALL)
            else:
                interleave(nc.vector.tensor_copy, hh_bf[k], fours[k], 0, NCALL)

        def second_product(t, k):
            banks, col = y_place[k]
            for g in range(G):
                product(banks[g][t], col, g, wo_codes, wo_scales, t, hh_codes[k], hh_scales[k], 0, NCALL)

        def squash(k0, k1):
            banks, col = y_place[k0]
            width = NCALL * (k1 - k0)
            lo = NCALL * (k0 % 2)
            for t in range(2):
                for g in range(G):
                    nc.scalar.activation(out=th[g][t][k0 // 2][:, lo:lo + width], in_=banks[g][t][:, col:col + width],
                                         func=ACT.Tanh, bias=ob_sb[:, 2 * g + t:2 * g + t + 1], scale=1.0)

        def finish(h):
            for t in range(2):
                for g in range(G):
                    nc.vector.tensor_scalar(out=res[g][t][h][:], in0=th[g][t][h][:],
                                            scalar1=osc_sb[:, 2 * g + t:2 * g + t + 1], scalar2=None, op0=ALU.mult)
                    nc.sync.dma_start(out=out[g, P * t:P * (t + 1), half(h)], in_=res[g][t][h][:])

        hh_words(0, True)
        hh_words(1, True)
        for k in range(2):
            quantize(hh_codes[k][:], hh_scales[k][:], hh_bf[k][:])
            for t in range(2):
                second_product(t, k)
        hh_words(2, True)
        hh_words(3, False)
        squash(0, 1)
        squash(1, 2)
        quantize(hh_codes[2][:], hh_scales[2][:], hh_bf[2][:])
        second_product(0, 2)
        quantize(hh_codes[3][:], hh_scales[3][:], hh_bf[3][:])
        second_product(0, 3)
        second_product(1, 2)
        second_product(1, 3)
        squash(2, 4)
        for h in range(2):
            finish(h)
